import numpy as np
import ml_dtypes


def mxq(x, axis, fmt="e4m3"):
    dtype, down = {"e4m3": (ml_dtypes.float8_e4m3fn, 7), "e5m2": (ml_dtypes.float8_e5m2, 14)}[fmt]
    v = np.moveaxis(np.asarray(x, np.float32).astype(ml_dtypes.bfloat16).astype(np.float64), axis, -1)
    blocks = v.reshape(v.shape[:-1] + (-1, 32))
    amax = np.abs(blocks).max(-1, keepdims=True)
    byte = np.maximum(np.where(amax > 0, np.frexp(amax)[1] - 1 + 127, 0) - down, 1)
    scale = np.exp2(byte - 127.0)
    codes = (blocks / scale).astype(np.float32).astype(dtype).astype(np.float64)
    return np.moveaxis((codes * scale).reshape(v.shape), -1, axis)


WIDE = False


def mx_kscale(k):
    if not WIDE:
        return np.ones(k)
    levels = np.array([10, -10, 5, -5, 0])
    if k % 512:
        return np.exp2(np.random.permutation(np.resize(levels, k // 32))).repeat(32)
    a = np.empty((k // 512, 16))
    for p in range(k // 512):
        a[p, :8] = np.random.permutation(np.resize(levels, 8))
        for g in range(8):
            far = levels[np.abs(levels - a[p, g]) >= 10]
            a[p, g + 8] = far[np.random.randint(len(far))]
    return np.exp2(a.ravel()).repeat(32)


def f64(x):
    return np.asarray(x).astype(np.float64)


def striped(idx):
    return np.tile(idx.reshape(-1, 16).T, (8, 1)).astype(np.uint16)


def unstriped(offs):
    return offs[:16].T.reshape(-1).astype(np.int64)


def striped8(idx):
    return np.concatenate([x.reshape(-1, 16).T for x in idx]).astype(np.uint16)


def runs(offs, k):
    lists = np.stack([offs[16 * r : 16 * r + 16].T.reshape(-1) for r in range(8)]).astype(np.int64)
    return lists[np.arange(k) % 512 // 64]


def pack_weight(w):
    k, n = w.shape
    w = f64(np.asarray(w, np.float32).astype(ml_dtypes.bfloat16)).reshape(k // 32, 32, n)
    amax = np.abs(w).max(1)
    byte = np.clip(np.where(amax > 0, np.frexp(amax)[1] - 1 + 127 - 7, 1), 1, 254)
    scaled = (w * np.exp2(127.0 - byte)[:, None, :]).reshape(k, n).astype(np.float32)
    words = np.ascontiguousarray(scaled.reshape(k // 512, 128, 4, n).transpose(0, 1, 3, 2)).astype(ml_dtypes.float8_e4m3fn).view(np.uint8)
    return words, np.ascontiguousarray(byte.astype(np.uint8).reshape(k // 512, 16, n))


def unpack_weight(words, scales):
    g, p, n, _ = words.shape
    vals = np.ascontiguousarray(words).view(ml_dtypes.float8_e4m3fn).astype(np.float64) * np.repeat(np.exp2(scales.astype(np.float64) - 127.0), 8, axis=1)[..., None]
    return vals.transpose(0, 1, 3, 2).reshape(g * 512, n)


K, T, S, H, G = 512, 2048, 512, 512, 2048


def setup_inputs():
    n = np.random.standard_normal
    s = mx_kscale(K)[:, None]
    packed_xT = pack_weight(n((K, T)) * s)
    packed_dT = pack_weight(n((K, G)) / s)
    return {
        "x_words": packed_xT[0],
        "x_scales": packed_xT[1],
        "w1": (n((K, H)) / np.sqrt(K) / s).astype(np.float32),
        "gs": (np.random.uniform(0.5, 1.5, (K, 1)) * s).astype(np.float32),
        "d_words": packed_dT[0],
        "d_scales": packed_dT[1],
        "tau": np.random.uniform(0.3, 0.9, (H, 1)).astype(np.float32),
        "offs": striped(np.random.permutation(T)[:S]),
        "n1": striped(np.random.permutation(S)),
        "n2": striped(np.random.permutation(S)),
        "k1": striped8(np.random.randint(0, G, (8, H))),
        "n3": striped(np.random.permutation(S)),
    }


def reference(x_words, x_scales, w1, gs, d_words, d_scales, tau, offs, n1, n2, k1, n3):
    d_k1 = unpack_weight(d_words, d_scales)[np.arange(K)[:, None], runs(k1, K)]
    xq = unpack_weight(x_words, x_scales)[:, unstriped(offs)]
    y = mxq(f64(w1), 0, "e4m3").T @ xq
    ex = np.exp(0.5 * y)
    z = f64(gs) * ((2.0 * ex) / (ex + ex[:, unstriped(n1)] + ex[:, unstriped(n2)]))
    h = 0.0625 * ((d_k1.T @ mxq(z, 0, "e4m3")))
    top = h.max(axis=1, keepdims=True)
    ea = np.exp(f64(tau) * (h[:, unstriped(n3)] - top))
    return 2.0 * (h * ea)

@@ -1,0 +1,173 @@
+from contextlib import ExitStack
+
+import concourse.mybir as mybir
+
+K, T, S, H, G = 512, 2048, 512, 512, 2048
+FLOPS = 2 * K * H * S * 2
+
+F32 = mybir.dt.float32
+BF16 = mybir.dt.bfloat16
+I32 = mybir.dt.int32
+U32 = mybir.dt.uint32
+U16 = mybir.dt.uint16
+U8 = mybir.dt.uint8
+FP8X4 = mybir.dt.float8_e4m3fn_x4
+ACT = mybir.ActivationFunctionType
+ALU = mybir.AluOpType
+
+P = 128
+PACK = 4
+LIST_COLS = S // 16
+PAD = 8
+CHUNK = 128
+CHUNKS = S // CHUNK
+HALF = S // 2
+W_SPLIT = 48
+
+
+def tile_picked_denseshareepk_none_p_kernel(
+    tc, x_words, x_scales, w1, gs, d_words, d_scales, tau, offs, n1, n2, k1, n3, out
+):
+    nc = tc.nc
+    with ExitStack() as ctx:
+        lists = ctx.enter_context(tc.tile_pool(name="lists", bufs=1))
+        sb = ctx.enter_context(tc.tile_pool(name="sb", bufs=1))
+        ps = ctx.enter_context(tc.psum_pool(name="ps", bufs=1))
+
+        def load_list(name, src):
+            t = lists.tile([P, LIST_COLS], U16, name=name)
+            nc.sync.dma_start(t[:], src)
+            return t
+
+        xs_tab = sb.tile([P, T], U8, name="xs_tab", align_bytes=64)
+        ds_tab = sb.tile([P, G], U8, name="ds_tab", align_bytes=64)
+        ds_placed = sb.tile([P, H], U8, name="ds_placed", align_bytes=64)
+        nc.gpsimd.memset(xs_tab[:].bitcast(I32), 0)
+        nc.vector.memset(ds_tab[:].bitcast(I32), 0)
+        nc.gpsimd.memset(ds_placed[:].bitcast(I32), 0)
+        ex = [sb.tile([P, S + PAD], F32, name=f"ex{t}", align_bytes=64) for t in range(PACK)]
+        for t in range(PACK):
+            nc.gpsimd.memset(ex[t][:, S:], 0.0)
+
+        w_raw = sb.tile([P, PACK, H], F32, name="w_raw", tag="big", align_bytes=64)
+        nc.sync.dma_start(w_raw[:], w1.rearrange("(p j) c -> p j c", j=PACK))
+        offs_t = load_list("offs_t", offs)
+        k1_t = load_list("k1_t", k1)
+        n1_t = load_list("n1_t", n1)
+        n2_t = load_list("n2_t", n2)
+        n3_t = load_list("n3_t", n3)
+        xw_tab = sb.tile([P, T], I32, name="xw_tab", align_bytes=64)
+        nc.sync.dma_start(xw_tab[:], x_words[0].rearrange("p n t -> p (n t)").bitcast(I32))
+        gs_t = sb.tile([P, PACK], F32, name="gs_t")
+        nc.sync.dma_start(gs_t[:], gs.rearrange("(p t) o -> p (t o)", t=PACK))
+        tau_t = sb.tile([P, PACK], F32, name="tau_t")
+        with nc.allow_non_contiguous_dma(reason="one rate a partition"):
+            nc.sync.dma_start(tau_t[:], tau.rearrange("(m p) o -> p (m o)", p=P))
+        for q in range(4):
+            nc.scalar.dma_start(
+                xs_tab[32 * q : 32 * q + 4, :].bitcast(I32), x_scales[0, 4 * q : 4 * q + 4, :].bitcast(I32)
+            )
+        nc.scalar.dma_start(ds_tab[0:P:8, :].bitcast(I32), d_scales[0].bitcast(I32))
+
+        xs_pick = sb.tile([P, S], U8, name="xs_pick", align_bytes=64)
+        nc.vector.tensor_copy(xs_pick[:], xs_tab[:].indirect(offs_t[:]))
+
+        w_bf = sb.tile([P, PACK * H], BF16, name="w_bf", align_bytes=64)
+        w_dst = w_bf[:].rearrange("p (t m j) -> p m j t", t=PACK, j=PACK)
+        w_src = w_raw[:].rearrange("p j (m t) -> p m j t", t=PACK)
+        nc.vector.tensor_copy(w_dst[:, :W_SPLIT], w_src[:, :W_SPLIT])
+        nc.scalar.copy(w_dst[:, W_SPLIT:], w_src[:, W_SPLIT:])
+        dw_tab = sb.tile([P, G], I32, name="dw_tab", tag="big", align_bytes=64)
+        nc.sync.dma_start(dw_tab[:], d_words[0].rearrange("p n t -> p (n t)").bitcast(I32))
+        w_codes = sb.tile([P, H], U32, name="w_codes", align_bytes=64)
+        w_sc = sb.tile([P, H], U8, name="w_sc", align_bytes=64)
+        nc.vector.quantize_mx(out=w_codes[:].bitcast(FP8X4), scales=w_sc[:], in_=w_bf[:])
+
+        xw_pick = sb.tile([P, S], U32, name="xw_pick", align_bytes=64)
+        for h in range(2):
+            nc.vector.tensor_copy(
+                xw_pick[:, h * HALF : (h + 1) * HALF],
+                xw_tab[:].bitcast(U32).indirect(offs_t[:, h * LIST_COLS // 2 : (h + 1) * LIST_COLS // 2]),
+            )
+        ds_pick = sb.tile([P, H], U8, name="ds_pick", align_bytes=64)
+        nc.vector.tensor_copy(ds_pick[:], ds_tab[:].indirect(k1_t[:]))
+        for q in range(4):
+            nc.sync.dma_start(
+                ds_placed[32 * q : 32 * q + 4, :].bitcast(I32), ds_pick[32 * q : 32 * q + 32 : 8, :].bitcast(I32)
+            )
+
+        den = sb.tile([P, PACK, S], F32, name="den", align_bytes=64)
+        first = sb.tile([P, PACK, S], F32, name="first", tag="four_planes", align_bytes=64)
+        for t in range(PACK):
+            y_ps = ps.tile([P, S], F32, name="y_ps", tag="y", bufs=2)
+            for h in range(2):
+                cols = slice(h * HALF, (h + 1) * HALF)
+                nc.tensor.matmul_mx(
+                    out=y_ps[:, cols],
+                    lhsT=w_codes[:, t * P : (t + 1) * P].bitcast(FP8X4),
+                    lhsT_scale=w_sc[:, t * P : (t + 1) * P],
+                    rhs=xw_pick[:, cols].bitcast(FP8X4),
+                    rhs_scale=xs_pick[:, cols],
+                    start=True,
+                    stop=True,
+                )
+            nc.scalar.activation(ex[t][:, :S], y_ps[:], ACT.Exp, scale=0.5)
+            nc.scalar.activation(first[:, t, :], ex[t][:].indirect(n1_t[:]), ACT.Copy)
+            both = sb.tile([P, S], F32, name=f"both{t}", tag=f"plane{t}", align_bytes=64)
+            nc.vector.tensor_tensor(both[:], ex[t][:].indirect(n2_t[:]), first[:, t, :], ALU.add)
+            nc.vector.tensor_tensor(den[:, t, :], both[:], ex[t][:, :S], ALU.add)
+        num = sb.tile([P, PACK, S], F32, name="num", tag="four_planes", align_bytes=64)
+        for t in range(PACK):
+            nc.vector.tensor_scalar(num[:, t, :], ex[t][:, :S], gs_t[:, t : t + 1], 2.0, ALU.mult, ALU.mult)
+        dw_pick = sb.tile([P, H], U32, name="dw_pick", tag=f"plane{PACK - 1}", align_bytes=64)
+        nc.vector.tensor_copy(dw_pick[:], dw_tab[:].bitcast(U32).indirect(k1_t[:]))
+
+        z_codes = sb.tile([P, S], U32, name="z_codes", align_bytes=64)
+        z_sc = sb.tile([P, S], U8, name="z_sc", align_bytes=64)
+        h_ps = [ps.tile([P, S], F32, name=f"h{m}") for m in range(H // P)]
+        root = sb.tile([P, PACK, S], F32, name="root")
+        nc.scalar.activation(root[:, :2, :], den[:, :2, :], ACT.Abs_reciprocal_sqrt)
+        for c in range(CHUNKS):
+            cols = slice(c * CHUNK, (c + 1) * CHUNK)
+            nc.scalar.activation(root[:, 2:, cols], den[:, 2:, cols], ACT.Abs_reciprocal_sqrt)
+            other = sb.tile([P, PACK, CHUNK], F32, name=f"other{c}")
+            nc.scalar.activation(other[:], root[:, :, cols], ACT.Square)
+            last = num[:, :, cols]
+            z_bf = sb.tile([P, PACK * CHUNK], BF16, name=f"z_bf{c}", align_bytes=64)
+            nc.vector.tensor_tensor(
+                z_bf[:].rearrange("p (c i t) -> p c t i", i=4, t=PACK),
+                other[:].rearrange("p t (c i) -> p c t i", i=4),
+                last.rearrange("p t (c i) -> p c t i", i=4),
+                ALU.mult,
+            )
+            nc.vector.quantize_mx(out=z_codes[:, cols].bitcast(FP8X4), scales=z_sc[:, cols], in_=z_bf[:])
+            for m in range(H // P):
+                nc.tensor.matmul_mx(
+                    out=h_ps[m][:, cols],
+                    lhsT=dw_pick[:, m * P : (m + 1) * P].bitcast(FP8X4),
+                    lhsT_scale=ds_placed[:, m * P : (m + 1) * P],
+                    rhs=z_codes[:, cols].bitcast(FP8X4),
+                    rhs_scale=z_sc[:, cols],
+                    start=True,
+                    stop=True,
+                )
+
+        for m in range(H // P):
+            h_sb = sb.tile([P, S], F32, name=f"h_sb{m}", align_bytes=64)
+            top = sb.tile([P, 1], F32, name=f"top{m}")
+            nc.vector.tensor_scalar(h_sb[:], h_ps[m][:], 0.0625, None, ALU.mult, ALU.max, accum_out=top[:])
+            shift = sb.tile([P, 1], F32, name=f"shift{m}")
+            nc.vector.tensor_scalar(shift[:], top[:], tau_t[:, m : m + 1], -1.0, ALU.mult, ALU.mult)
+            for h in range(2):
+                cols = slice(h * HALF, (h + 1) * HALF)
+                ea = sb.tile([P, HALF], F32, name=f"ea{m}_{h}")
+                nc.scalar.activation(
+                    ea[:],
+                    h_sb[:].indirect(n3_t[:, h * LIST_COLS // 2 : (h + 1) * LIST_COLS // 2]),
+                    ACT.Exp,
+                    bias=shift[:],
+                    scale=tau_t[:, m : m + 1],
+                )
+                res = sb.tile([P, HALF], F32, name=f"res{m}_{h}")
+                nc.vector.scalar_tensor_tensor(res[:], h_sb[:, cols], 2.0, ea[:], ALU.mult, ALU.mult)
+                nc.sync.dma_start(out[m * P : (m + 1) * P, cols], res[:])

@@ -22,6 +22,8 @@ PAD = 8
 CHUNK = 128
 CHUNKS = S // CHUNK
 HALF = S // 2
+EARLY = 2
+LAST = 128
 W_SPLIT = 48
 
 
@@ -49,25 +51,28 @@ def tile_picked_denseshareepk_none_p_kernel(
         for t in range(PACK):
             nc.gpsimd.memset(ex[t][:, S:], 0.0)
 
-        w_raw = sb.tile([P, PACK, H], F32, name="w_raw", tag="big", align_bytes=64)
-        nc.sync.dma_start(w_raw[:], w1.rearrange("(p j) c -> p j c", j=PACK))
         offs_t = load_list("offs_t", offs)
         k1_t = load_list("k1_t", k1)
+        w_raw = sb.tile([P, PACK, H], F32, name="w_raw", align_bytes=64)
+        nc.sync.dma_start(w_raw[:], w1.rearrange("(p j) c -> p j c", j=PACK))
         n1_t = load_list("n1_t", n1)
+        for q in range(4):
+            nc.sync.dma_start(
+                xs_tab[32 * q : 32 * q + 4, :].bitcast(I32), x_scales[0, 4 * q : 4 * q + 4, :].bitcast(I32)
+            )
         n2_t = load_list("n2_t", n2)
-        n3_t = load_list("n3_t", n3)
-        xw_tab = sb.tile([P, T], I32, name="xw_tab", align_bytes=64)
+        xw_tab = sb.tile([P, T], I32, name="xw_tab", tag="x_table", align_bytes=64)
         nc.sync.dma_start(xw_tab[:], x_words[0].rearrange("p n t -> p (n t)").bitcast(I32))
+        nc.sync.dma_start(ds_tab[0:P:8, :].bitcast(I32), d_scales[0].bitcast(I32))
+        n3_t = load_list("n3_t", n3)
         gs_t = sb.tile([P, PACK], F32, name="gs_t")
         nc.sync.dma_start(gs_t[:], gs.rearrange("(p t) o -> p (t o)", t=PACK))
+
+        dw_tab = sb.tile([P, G], I32, name="dw_tab", tag="d_table", align_bytes=64)
+        nc.sync.dma_start(dw_tab[:], d_words[0].rearrange("p n t -> p (n t)").bitcast(I32))
         tau_t = sb.tile([P, PACK], F32, name="tau_t")
         with nc.allow_non_contiguous_dma(reason="one rate a partition"):
             nc.sync.dma_start(tau_t[:], tau.rearrange("(m p) o -> p (m o)", p=P))
-        for q in range(4):
-            nc.scalar.dma_start(
-                xs_tab[32 * q : 32 * q + 4, :].bitcast(I32), x_scales[0, 4 * q : 4 * q + 4, :].bitcast(I32)
-            )
-        nc.scalar.dma_start(ds_tab[0:P:8, :].bitcast(I32), d_scales[0].bitcast(I32))
 
         xs_pick = sb.tile([P, S], U8, name="xs_pick", align_bytes=64)
         nc.vector.tensor_copy(xs_pick[:], xs_tab[:].indirect(offs_t[:]))
@@ -77,8 +82,6 @@ def tile_picked_denseshareepk_none_p_kernel(
         w_src = w_raw[:].rearrange("p j (m t) -> p m j t", t=PACK)
         nc.vector.tensor_copy(w_dst[:, :W_SPLIT], w_src[:, :W_SPLIT])
         nc.scalar.copy(w_dst[:, W_SPLIT:], w_src[:, W_SPLIT:])
-        dw_tab = sb.tile([P, G], I32, name="dw_tab", tag="big", align_bytes=64)
-        nc.sync.dma_start(dw_tab[:], d_words[0].rearrange("p n t -> p (n t)").bitcast(I32))
         w_codes = sb.tile([P, H], U32, name="w_codes", align_bytes=64)
         w_sc = sb.tile([P, H], U8, name="w_sc", align_bytes=64)
         nc.vector.quantize_mx(out=w_codes[:].bitcast(FP8X4), scales=w_sc[:], in_=w_bf[:])
@@ -89,17 +92,21 @@ def tile_picked_denseshareepk_none_p_kernel(
                 xw_pick[:, h * HALF : (h + 1) * HALF],
                 xw_tab[:].bitcast(U32).indirect(offs_t[:, h * LIST_COLS // 2 : (h + 1) * LIST_COLS // 2]),
             )
-        ds_pick = sb.tile([P, H], U8, name="ds_pick", align_bytes=64)
+        ds_pick = sb.tile([P, H], U8, name="ds_pick", tag="x_table", align_bytes=64)
         nc.vector.tensor_copy(ds_pick[:], ds_tab[:].indirect(k1_t[:]))
         for q in range(4):
             nc.sync.dma_start(
                 ds_placed[32 * q : 32 * q + 4, :].bitcast(I32), ds_pick[32 * q : 32 * q + 32 : 8, :].bitcast(I32)
             )
 
+        dw_pick = sb.tile([P, H], U32, name="dw_pick", align_bytes=64)
+        nc.vector.tensor_copy(dw_pick[:], dw_tab[:].bitcast(U32).indirect(k1_t[:]))
+        num = sb.tile([P, PACK, S], F32, name="num", align_bytes=64)
+        both = sb.tile([P, PACK, S], F32, name="both", tag="d_table", align_bytes=64)
         den = sb.tile([P, PACK, S], F32, name="den", align_bytes=64)
-        first = sb.tile([P, PACK, S], F32, name="first", tag="four_planes", align_bytes=64)
+        first = sb.tile([P, PACK, S], F32, name="first", align_bytes=64)
         for t in range(PACK):
-            y_ps = ps.tile([P, S], F32, name="y_ps", tag="y", bufs=2)
+            y_ps = ps.tile([P, S], F32, name="y_ps", tag="y", bufs=PACK)
             for h in range(2):
                 cols = slice(h * HALF, (h + 1) * HALF)
                 nc.tensor.matmul_mx(
@@ -112,32 +119,28 @@ def tile_picked_denseshareepk_none_p_kernel(
                     stop=True,
                 )
             nc.scalar.activation(ex[t][:, :S], y_ps[:], ACT.Exp, scale=0.5)
-            nc.scalar.activation(first[:, t, :], ex[t][:].indirect(n1_t[:]), ACT.Copy)
-            both = sb.tile([P, S], F32, name=f"both{t}", tag=f"plane{t}", align_bytes=64)
-            nc.vector.tensor_tensor(both[:], ex[t][:].indirect(n2_t[:]), first[:, t, :], ALU.add)
-            nc.vector.tensor_tensor(den[:, t, :], both[:], ex[t][:, :S], ALU.add)
-        num = sb.tile([P, PACK, S], F32, name="num", tag="four_planes", align_bytes=64)
-        for t in range(PACK):
             nc.vector.tensor_scalar(num[:, t, :], ex[t][:, :S], gs_t[:, t : t + 1], 2.0, ALU.mult, ALU.mult)
-        dw_pick = sb.tile([P, H], U32, name="dw_pick", tag=f"plane{PACK - 1}", align_bytes=64)
-        nc.vector.tensor_copy(dw_pick[:], dw_tab[:].bitcast(U32).indirect(k1_t[:]))
-
+            nc.scalar.activation(first[:, t, :], ex[t][:].indirect(n1_t[:]), ACT.Copy)
+            nc.vector.tensor_tensor(both[:, t, :], ex[t][:].indirect(n2_t[:]), first[:, t, :], ALU.add)
+            nc.vector.tensor_tensor(den[:, t, :], both[:, t, :], ex[t][:, :S], ALU.add)
         z_codes = sb.tile([P, S], U32, name="z_codes", align_bytes=64)
         z_sc = sb.tile([P, S], U8, name="z_sc", align_bytes=64)
         h_ps = [ps.tile([P, S], F32, name=f"h{m}") for m in range(H // P)]
         root = sb.tile([P, PACK, S], F32, name="root")
-        nc.scalar.activation(root[:, :2, :], den[:, :2, :], ACT.Abs_reciprocal_sqrt)
+        recip = sb.tile([P, PACK, S], F32, name="recip")
+        for t in range(EARLY):
+            nc.scalar.activation(root[:, t, :], den[:, t, :], ACT.Abs_reciprocal_sqrt)
+        for t in range(EARLY):
+            nc.scalar.activation(recip[:, t, :], root[:, t, :], ACT.Square)
         for c in range(CHUNKS):
             cols = slice(c * CHUNK, (c + 1) * CHUNK)
-            nc.scalar.activation(root[:, 2:, cols], den[:, 2:, cols], ACT.Abs_reciprocal_sqrt)
-            other = sb.tile([P, PACK, CHUNK], F32, name=f"other{c}")
-            nc.scalar.activation(other[:], root[:, :, cols], ACT.Square)
-            last = num[:, :, cols]
+            nc.scalar.activation(root[:, EARLY:, cols], den[:, EARLY:, cols], ACT.Abs_reciprocal_sqrt)
+            nc.scalar.activation(recip[:, EARLY:, cols], root[:, EARLY:, cols], ACT.Square)
             z_bf = sb.tile([P, PACK * CHUNK], BF16, name=f"z_bf{c}", align_bytes=64)
             nc.vector.tensor_tensor(
                 z_bf[:].rearrange("p (c i t) -> p c t i", i=4, t=PACK),
-                other[:].rearrange("p t (c i) -> p c t i", i=4),
-                last.rearrange("p t (c i) -> p c t i", i=4),
+                recip[:, :, cols].rearrange("p t (c i) -> p c t i", i=4),
+                num[:, :, cols].rearrange("p t (c i) -> p c t i", i=4),
                 ALU.mult,
             )
             nc.vector.quantize_mx(out=z_codes[:, cols].bitcast(FP8X4), scales=z_sc[:, cols], in_=z_bf[:])
@@ -152,22 +155,23 @@ def tile_picked_denseshareepk_none_p_kernel(
                     stop=True,
                 )
 
-        for m in range(H // P):
+        blocks = H // P
+        for m in range(blocks):
             h_sb = sb.tile([P, S], F32, name=f"h_sb{m}", align_bytes=64)
             top = sb.tile([P, 1], F32, name=f"top{m}")
             nc.vector.tensor_scalar(h_sb[:], h_ps[m][:], 0.0625, None, ALU.mult, ALU.max, accum_out=top[:])
             shift = sb.tile([P, 1], F32, name=f"shift{m}")
             nc.vector.tensor_scalar(shift[:], top[:], tau_t[:, m : m + 1], -1.0, ALU.mult, ALU.mult)
-            for h in range(2):
-                cols = slice(h * HALF, (h + 1) * HALF)
-                ea = sb.tile([P, HALF], F32, name=f"ea{m}_{h}")
+            edges = (0, HALF, S) if m < blocks - 1 else (0, HALF, S - LAST, S)
+            for lo, hi in zip(edges, edges[1:]):
+                ea = sb.tile([P, hi - lo], F32, name=f"ea{m}_{lo}")
                 nc.scalar.activation(
                     ea[:],
-                    h_sb[:].indirect(n3_t[:, h * LIST_COLS // 2 : (h + 1) * LIST_COLS // 2]),
+                    h_sb[:].indirect(n3_t[:, lo // 16 : hi // 16]),
                     ACT.Exp,
                     bias=shift[:],
                     scale=tau_t[:, m : m + 1],
                 )
-                res = sb.tile([P, HALF], F32, name=f"res{m}_{h}")
-                nc.vector.scalar_tensor_tensor(res[:], h_sb[:, cols], 2.0, ea[:], ALU.mult, ALU.mult)
-                nc.sync.dma_start(out[m * P : (m + 1) * P, cols], res[:])
+                res = sb.tile([P, hi - lo], F32, name=f"res{m}_{lo}")
+                nc.vector.scalar_tensor_tensor(res[:], h_sb[:, lo:hi], 2.0, ea[:], ALU.mult, ALU.mult)
+                nc.sync.dma_start(out[m * P : (m + 1) * P, lo:hi], res[:])

@@ -24,7 +24,6 @@ CHUNKS = S // CHUNK
 HALF = S // 2
 EARLY = 2
 LAST = 128
-W_SPLIT = 48
 
 
 def tile_picked_denseshareepk_none_p_kernel(
@@ -68,7 +67,7 @@ def tile_picked_denseshareepk_none_p_kernel(
         gs_t = sb.tile([P, PACK], F32, name="gs_t")
         nc.sync.dma_start(gs_t[:], gs.rearrange("(p t) o -> p (t o)", t=PACK))
 
-        dw_tab = sb.tile([P, G], I32, name="dw_tab", tag="d_table", align_bytes=64)
+        dw_tab = sb.tile([P, G], I32, name="dw_tab", align_bytes=64)
         nc.sync.dma_start(dw_tab[:], d_words[0].rearrange("p n t -> p (n t)").bitcast(I32))
         tau_t = sb.tile([P, PACK], F32, name="tau_t")
         with nc.allow_non_contiguous_dma(reason="one rate a partition"):
@@ -77,14 +76,14 @@ def tile_picked_denseshareepk_none_p_kernel(
         xs_pick = sb.tile([P, S], U8, name="xs_pick", align_bytes=64)
         nc.vector.tensor_copy(xs_pick[:], xs_tab[:].indirect(offs_t[:]))
 
-        w_bf = sb.tile([P, PACK * H], BF16, name="w_bf", align_bytes=64)
-        w_dst = w_bf[:].rearrange("p (t m j) -> p m j t", t=PACK, j=PACK)
-        w_src = w_raw[:].rearrange("p j (m t) -> p m j t", t=PACK)
-        nc.vector.tensor_copy(w_dst[:, :W_SPLIT], w_src[:, :W_SPLIT])
-        nc.scalar.copy(w_dst[:, W_SPLIT:], w_src[:, W_SPLIT:])
         w_codes = sb.tile([P, H], U32, name="w_codes", align_bytes=64)
         w_sc = sb.tile([P, H], U8, name="w_sc", align_bytes=64)
-        nc.vector.quantize_mx(out=w_codes[:].bitcast(FP8X4), scales=w_sc[:], in_=w_bf[:])
+        w_src = w_raw[:].rearrange("p j (m t) -> p m j t", t=PACK)
+        for pair, round_copy in enumerate((nc.vector.tensor_copy, nc.scalar.copy)):
+            w_bf = sb.tile([P, 2 * H], BF16, name=f"w_bf{pair}", align_bytes=64)
+            round_copy(w_bf[:].rearrange("p (t m j) -> p m j t", t=2, j=PACK), w_src[:, :, :, 2 * pair : 2 * pair + 2])
+            cols = slice(2 * P * pair, 2 * P * (pair + 1))
+            nc.vector.quantize_mx(out=w_codes[:, cols].bitcast(FP8X4), scales=w_sc[:, cols], in_=w_bf[:])
 
         xw_pick = sb.tile([P, S], U32, name="xw_pick", align_bytes=64)
         for h in range(2):
@@ -101,52 +100,96 @@ def tile_picked_denseshareepk_none_p_kernel(
 
         dw_pick = sb.tile([P, H], U32, name="dw_pick", align_bytes=64)
         nc.vector.tensor_copy(dw_pick[:], dw_tab[:].bitcast(U32).indirect(k1_t[:]))
-        num = sb.tile([P, PACK, S], F32, name="num", align_bytes=64)
-        both = sb.tile([P, PACK, S], F32, name="both", tag="d_table", align_bytes=64)
+        right = sb.tile([P, PACK, S], F32, name="right", align_bytes=64)
+        both = sb.tile([P, PACK, S], F32, name="both", align_bytes=64)
         den = sb.tile([P, PACK, S], F32, name="den", align_bytes=64)
         first = sb.tile([P, PACK, S], F32, name="first", align_bytes=64)
-        for t in range(PACK):
-            y_ps = ps.tile([P, S], F32, name="y_ps", tag="y", bufs=PACK)
-            for h in range(2):
-                cols = slice(h * HALF, (h + 1) * HALF)
-                nc.tensor.matmul_mx(
-                    out=y_ps[:, cols],
-                    lhsT=w_codes[:, t * P : (t + 1) * P].bitcast(FP8X4),
-                    lhsT_scale=w_sc[:, t * P : (t + 1) * P],
-                    rhs=xw_pick[:, cols].bitcast(FP8X4),
-                    rhs_scale=xs_pick[:, cols],
-                    start=True,
-                    stop=True,
-                )
+
+        def project(dst, t, cols):
+            nc.tensor.matmul_mx(
+                out=dst,
+                lhsT=w_codes[:, t * P : (t + 1) * P].bitcast(FP8X4),
+                lhsT_scale=w_sc[:, t * P : (t + 1) * P],
+                rhs=xw_pick[:, cols].bitcast(FP8X4),
+                rhs_scale=xs_pick[:, cols],
+                start=True,
+                stop=True,
+            )
+
+        def early_exponentials(h):
+            cols = slice(h * HALF, (h + 1) * HALF)
+            y_ps = ps.tile([P, EARLY, HALF], F32, name="y_early", tag="y", bufs=PACK)
+            for t in range(EARLY):
+                project(y_ps[:, t, :], t, cols)
+            for t in range(EARLY):
+                nc.scalar.activation(ex[t][:, cols], y_ps[:, t, :], ACT.Exp, scale=0.5)
+
+        def late_exponential(t):
+            y_ps = ps.tile([P, S], F32, name="y_late", tag="y", bufs=PACK)
+            project(y_ps[:], t, slice(0, S))
             nc.scalar.activation(ex[t][:, :S], y_ps[:], ACT.Exp, scale=0.5)
-            nc.vector.tensor_scalar(num[:, t, :], ex[t][:, :S], gs_t[:, t : t + 1], 2.0, ALU.mult, ALU.mult)
+
+        def numerator(t):
+            nc.vector.tensor_scalar(right[:, t, :], ex[t][:, :S], gs_t[:, t : t + 1], None, ALU.mult)
+
+        def fetch_first(t):
             nc.scalar.activation(first[:, t, :], ex[t][:].indirect(n1_t[:]), ACT.Copy)
+
+        def fetch_second(t):
             nc.vector.tensor_tensor(both[:, t, :], ex[t][:].indirect(n2_t[:]), first[:, t, :], ALU.add)
+
+        def denominator(t):
             nc.vector.tensor_tensor(den[:, t, :], both[:, t, :], ex[t][:, :S], ALU.add)
+
+        for h in range(2):
+            early_exponentials(h)
+        for t in range(PACK):
+            fetch_first(t)
+            if t + EARLY < PACK:
+                late_exponential(t + EARLY)
+        for t in range(EARLY):
+            fetch_second(t)
+            numerator(t + EARLY)
+            denominator(t)
+        for t in range(EARLY, PACK):
+            fetch_second(t)
+        for t in range(EARLY, PACK):
+            denominator(t)
+
         z_codes = sb.tile([P, S], U32, name="z_codes", align_bytes=64)
         z_sc = sb.tile([P, S], U8, name="z_sc", align_bytes=64)
         h_ps = [ps.tile([P, S], F32, name=f"h{m}") for m in range(H // P)]
-        root = sb.tile([P, PACK, S], F32, name="root")
-        recip = sb.tile([P, PACK, S], F32, name="recip")
+        h_last = ps.tile([P, CHUNK], F32, name="h_last", tag="y", bufs=PACK)
+        left = sb.tile([P, PACK, S], F32, name="left")
+        root = sb.tile([P, PACK - EARLY, S], F32, name="root")
         for t in range(EARLY):
-            nc.scalar.activation(root[:, t, :], den[:, t, :], ACT.Abs_reciprocal_sqrt)
-        for t in range(EARLY):
-            nc.scalar.activation(recip[:, t, :], root[:, t, :], ACT.Square)
-        for c in range(CHUNKS):
+            nc.scalar.activation(left[:, t, :], den[:, t, :], ACT.Abs_reciprocal_sqrt, scale=0.5)
+            nc.vector.scalar_tensor_tensor(
+                right[:, t, :], left[:, t, :], gs_t[:, t : t + 1], ex[t][:, :S], ALU.mult, ALU.mult
+            )
+
+        def late_root(c):
             cols = slice(c * CHUNK, (c + 1) * CHUNK)
-            nc.scalar.activation(root[:, EARLY:, cols], den[:, EARLY:, cols], ACT.Abs_reciprocal_sqrt)
-            nc.scalar.activation(recip[:, EARLY:, cols], root[:, EARLY:, cols], ACT.Square)
+            nc.scalar.activation(root[:, :, cols], den[:, EARLY:, cols], ACT.Abs_reciprocal_sqrt, scale=0.5)
+
+        def share(c):
+            cols = slice(c * CHUNK, (c + 1) * CHUNK)
+            nc.scalar.activation(left[:, EARLY:, cols], root[:, :, cols], ACT.Square)
             z_bf = sb.tile([P, PACK * CHUNK], BF16, name=f"z_bf{c}", align_bytes=64)
             nc.vector.tensor_tensor(
                 z_bf[:].rearrange("p (c i t) -> p c t i", i=4, t=PACK),
-                recip[:, :, cols].rearrange("p t (c i) -> p c t i", i=4),
-                num[:, :, cols].rearrange("p t (c i) -> p c t i", i=4),
+                left[:, :, cols].rearrange("p t (c i) -> p c t i", i=4),
+                right[:, :, cols].rearrange("p t (c i) -> p c t i", i=4),
                 ALU.mult,
             )
+            return z_bf
+
+        def second_product(c, z_bf):
+            cols = slice(c * CHUNK, (c + 1) * CHUNK)
             nc.vector.quantize_mx(out=z_codes[:, cols].bitcast(FP8X4), scales=z_sc[:, cols], in_=z_bf[:])
             for m in range(H // P):
                 nc.tensor.matmul_mx(
-                    out=h_ps[m][:, cols],
+                    out=h_last[:] if (m, c) == (0, CHUNKS - 1) else h_ps[m][:, cols],
                     lhsT=dw_pick[:, m * P : (m + 1) * P].bitcast(FP8X4),
                     lhsT_scale=ds_placed[:, m * P : (m + 1) * P],
                     rhs=z_codes[:, cols].bitcast(FP8X4),
@@ -155,13 +198,38 @@ def tile_picked_denseshareepk_none_p_kernel(
                     stop=True,
                 )
 
+        late_root(0)
+        rounded = []
+        for c in range(CHUNKS):
+            if c + 1 < CHUNKS:
+                late_root(c + 1)
+            rounded.append(share(c))
+            if c > 0:
+                second_product(c - 1, rounded[c - 1])
+        second_product(CHUNKS - 1, rounded[-1])
+
         blocks = H // P
+        h_rows, shifts = [], []
         for m in range(blocks):
             h_sb = sb.tile([P, S], F32, name=f"h_sb{m}", align_bytes=64)
             top = sb.tile([P, 1], F32, name=f"top{m}")
-            nc.vector.tensor_scalar(h_sb[:], h_ps[m][:], 0.0625, None, ALU.mult, ALU.max, accum_out=top[:])
+            if m == 0:
+                kept = S - CHUNK
+                top_early = sb.tile([P, 1], F32, name="top_early")
+                nc.vector.tensor_scalar(
+                    h_sb[:, :kept], h_ps[m][:, :kept], 0.0625, None, ALU.mult, ALU.max, accum_out=top_early[:]
+                )
+                nc.vector.tensor_scalar(
+                    h_sb[:, kept:], h_last[:], 0.0625, top_early[:], ALU.mult, ALU.max, accum_out=top[:]
+                )
+            else:
+                nc.vector.tensor_scalar(h_sb[:], h_ps[m][:], 0.0625, None, ALU.mult, ALU.max, accum_out=top[:])
             shift = sb.tile([P, 1], F32, name=f"shift{m}")
             nc.vector.tensor_scalar(shift[:], top[:], tau_t[:, m : m + 1], -1.0, ALU.mult, ALU.mult)
+            h_rows.append(h_sb)
+            shifts.append(shift)
+        for m in range(blocks):
+            h_sb, shift = h_rows[m], shifts[m]
             edges = (0, HALF, S) if m < blocks - 1 else (0, HALF, S - LAST, S)
             for lo, hi in zip(edges, edges[1:]):
                 ea = sb.tile([P, hi - lo], F32, name=f"ea{m}_{lo}")

from contextlib import ExitStack

import concourse.mybir as mybir

K, T, S, H, G = 512, 2048, 512, 512, 2048
FLOPS = 2 * K * H * S * 2

F32 = mybir.dt.float32
BF16 = mybir.dt.bfloat16
I32 = mybir.dt.int32
U32 = mybir.dt.uint32
U16 = mybir.dt.uint16
U8 = mybir.dt.uint8
FP8X4 = mybir.dt.float8_e4m3fn_x4
ACT = mybir.ActivationFunctionType
ALU = mybir.AluOpType

P = 128
PACK = 4
LIST_COLS = S // 16
PAD = 8
CHUNK = 128
CHUNKS = S // CHUNK
HALF = S // 2
EARLY = 2
LAST = 128


def tile_picked_denseshareepk_none_p_kernel(
    tc, x_words, x_scales, w1, gs, d_words, d_scales, tau, offs, n1, n2, k1, n3, out
):
    nc = tc.nc
    with ExitStack() as ctx:
        lists = ctx.enter_context(tc.tile_pool(name="lists", bufs=1))
        sb = ctx.enter_context(tc.tile_pool(name="sb", bufs=1))
        ps = ctx.enter_context(tc.psum_pool(name="ps", bufs=1))

        def load_list(name, src):
            t = lists.tile([P, LIST_COLS], U16, name=name)
            nc.sync.dma_start(t[:], src)
            return t

        xs_tab = sb.tile([P, T], U8, name="xs_tab", align_bytes=64)
        ds_tab = sb.tile([P, G], U8, name="ds_tab", align_bytes=64)
        ds_placed = sb.tile([P, H], U8, name="ds_placed", align_bytes=64)
        nc.gpsimd.memset(xs_tab[:].bitcast(I32), 0)
        nc.vector.memset(ds_tab[:].bitcast(I32), 0)
        nc.gpsimd.memset(ds_placed[:].bitcast(I32), 0)
        ex = [sb.tile([P, S + PAD], F32, name=f"ex{t}", align_bytes=64) for t in range(PACK)]
        for t in range(PACK):
            nc.gpsimd.memset(ex[t][:, S:], 0.0)

        offs_t = load_list("offs_t", offs)
        k1_t = load_list("k1_t", k1)
        w_raw = sb.tile([P, PACK, H], F32, name="w_raw", align_bytes=64)
        nc.sync.dma_start(w_raw[:], w1.rearrange("(p j) c -> p j c", j=PACK))
        n1_t = load_list("n1_t", n1)
        for q in range(4):
            nc.sync.dma_start(
                xs_tab[32 * q : 32 * q + 4, :].bitcast(I32), x_scales[0, 4 * q : 4 * q + 4, :].bitcast(I32)
            )
        n2_t = load_list("n2_t", n2)
        xw_tab = sb.tile([P, T], I32, name="xw_tab", tag="x_table", align_bytes=64)
        nc.sync.dma_start(xw_tab[:], x_words[0].rearrange("p n t -> p (n t)").bitcast(I32))
        nc.sync.dma_start(ds_tab[0:P:8, :].bitcast(I32), d_scales[0].bitcast(I32))
        n3_t = load_list("n3_t", n3)
        gs_t = sb.tile([P, PACK], F32, name="gs_t")
        nc.sync.dma_start(gs_t[:], gs.rearrange("(p t) o -> p (t o)", t=PACK))

        dw_tab = sb.tile([P, G], I32, name="dw_tab", align_bytes=64)
        nc.sync.dma_start(dw_tab[:], d_words[0].rearrange("p n t -> p (n t)").bitcast(I32))
        tau_t = sb.tile([P, PACK], F32, name="tau_t")
        with nc.allow_non_contiguous_dma(reason="one rate a partition"):
            nc.sync.dma_start(tau_t[:], tau.rearrange("(m p) o -> p (m o)", p=P))

        xs_pick = sb.tile([P, S], U8, name="xs_pick", align_bytes=64)
        nc.vector.tensor_copy(xs_pick[:], xs_tab[:].indirect(offs_t[:]))

        w_codes = sb.tile([P, H], U32, name="w_codes", align_bytes=64)
        w_sc = sb.tile([P, H], U8, name="w_sc", align_bytes=64)
        w_src = w_raw[:].rearrange("p j (m t) -> p m j t", t=PACK)
        for pair, round_copy in enumerate((nc.vector.tensor_copy, nc.scalar.copy)):
            w_bf = sb.tile([P, 2 * H], BF16, name=f"w_bf{pair}", align_bytes=64)
            round_copy(w_bf[:].rearrange("p (t m j) -> p m j t", t=2, j=PACK), w_src[:, :, :, 2 * pair : 2 * pair + 2])
            cols = slice(2 * P * pair, 2 * P * (pair + 1))
            nc.vector.quantize_mx(out=w_codes[:, cols].bitcast(FP8X4), scales=w_sc[:, cols], in_=w_bf[:])

        xw_pick = sb.tile([P, S], U32, name="xw_pick", align_bytes=64)
        for h in range(2):
            nc.vector.tensor_copy(
                xw_pick[:, h * HALF : (h + 1) * HALF],
                xw_tab[:].bitcast(U32).indirect(offs_t[:, h * LIST_COLS // 2 : (h + 1) * LIST_COLS // 2]),
            )
        ds_pick = sb.tile([P, H], U8, name="ds_pick", tag="x_table", align_bytes=64)
        nc.vector.tensor_copy(ds_pick[:], ds_tab[:].indirect(k1_t[:]))
        for q in range(4):
            nc.sync.dma_start(
                ds_placed[32 * q : 32 * q + 4, :].bitcast(I32), ds_pick[32 * q : 32 * q + 32 : 8, :].bitcast(I32)
            )

        dw_pick = sb.tile([P, H], U32, name="dw_pick", align_bytes=64)
        nc.vector.tensor_copy(dw_pick[:], dw_tab[:].bitcast(U32).indirect(k1_t[:]))
        right = sb.tile([P, PACK, S], F32, name="right", align_bytes=64)
        both = sb.tile([P, PACK, S], F32, name="both", align_bytes=64)
        den = sb.tile([P, PACK, S], F32, name="den", align_bytes=64)
        first = sb.tile([P, PACK, S], F32, name="first", align_bytes=64)

        def project(dst, t, cols):
            nc.tensor.matmul_mx(
                out=dst,
                lhsT=w_codes[:, t * P : (t + 1) * P].bitcast(FP8X4),
                lhsT_scale=w_sc[:, t * P : (t + 1) * P],
                rhs=xw_pick[:, cols].bitcast(FP8X4),
                rhs_scale=xs_pick[:, cols],
                start=True,
                stop=True,
            )

        def early_exponentials(h):
            cols = slice(h * HALF, (h + 1) * HALF)
            y_ps = ps.tile([P, EARLY, HALF], F32, name="y_early", tag="y", bufs=PACK)
            for t in range(EARLY):
                project(y_ps[:, t, :], t, cols)
            for t in range(EARLY):
                nc.scalar.activation(ex[t][:, cols], y_ps[:, t, :], ACT.Exp, scale=0.5)

        def late_exponential(t):
            y_ps = ps.tile([P, S], F32, name="y_late", tag="y", bufs=PACK)
            project(y_ps[:], t, slice(0, S))
            nc.scalar.activation(ex[t][:, :S], y_ps[:], ACT.Exp, scale=0.5)

        def numerator(t):
            nc.vector.tensor_scalar(right[:, t, :], ex[t][:, :S], gs_t[:, t : t + 1], None, ALU.mult)

        def fetch_first(t):
            nc.scalar.activation(first[:, t, :], ex[t][:].indirect(n1_t[:]), ACT.Copy)

        def fetch_second(t):
            nc.vector.tensor_tensor(both[:, t, :], ex[t][:].indirect(n2_t[:]), first[:, t, :], ALU.add)

        def denominator(t):
            nc.vector.tensor_tensor(den[:, t, :], both[:, t, :], ex[t][:, :S], ALU.add)

        for h in range(2):
            early_exponentials(h)
        for t in range(PACK):
            fetch_first(t)
            if t + EARLY < PACK:
                late_exponential(t + EARLY)
        for t in range(EARLY):
            fetch_second(t)
            numerator(t + EARLY)
            denominator(t)
        for t in range(EARLY, PACK):
            fetch_second(t)
        for t in range(EARLY, PACK):
            denominator(t)

        z_codes = sb.tile([P, S], U32, name="z_codes", align_bytes=64)
        z_sc = sb.tile([P, S], U8, name="z_sc", align_bytes=64)
        h_ps = [ps.tile([P, S], F32, name=f"h{m}") for m in range(H // P)]
        h_last = ps.tile([P, CHUNK], F32, name="h_last", tag="y", bufs=PACK)
        left = sb.tile([P, PACK, S], F32, name="left")
        root = sb.tile([P, PACK - EARLY, S], F32, name="root")
        for t in range(EARLY):
            nc.scalar.activation(left[:, t, :], den[:, t, :], ACT.Abs_reciprocal_sqrt, scale=0.5)
            nc.vector.scalar_tensor_tensor(
                right[:, t, :], left[:, t, :], gs_t[:, t : t + 1], ex[t][:, :S], ALU.mult, ALU.mult
            )

        def late_root(c):
            cols = slice(c * CHUNK, (c + 1) * CHUNK)
            nc.scalar.activation(root[:, :, cols], den[:, EARLY:, cols], ACT.Abs_reciprocal_sqrt, scale=0.5)

        def share(c):
            cols = slice(c * CHUNK, (c + 1) * CHUNK)
            nc.scalar.activation(left[:, EARLY:, cols], root[:, :, cols], ACT.Square)
            z_bf = sb.tile([P, PACK * CHUNK], BF16, name=f"z_bf{c}", align_bytes=64)
            nc.vector.tensor_tensor(
                z_bf[:].rearrange("p (c i t) -> p c t i", i=4, t=PACK),
                left[:, :, cols].rearrange("p t (c i) -> p c t i", i=4),
                right[:, :, cols].rearrange("p t (c i) -> p c t i", i=4),
                ALU.mult,
            )
            return z_bf

        def second_product(c, z_bf):
            cols = slice(c * CHUNK, (c + 1) * CHUNK)
            nc.vector.quantize_mx(out=z_codes[:, cols].bitcast(FP8X4), scales=z_sc[:, cols], in_=z_bf[:])
            for m in range(H // P):
                nc.tensor.matmul_mx(
                    out=h_last[:] if (m, c) == (0, CHUNKS - 1) else h_ps[m][:, cols],
                    lhsT=dw_pick[:, m * P : (m + 1) * P].bitcast(FP8X4),
                    lhsT_scale=ds_placed[:, m * P : (m + 1) * P],
                    rhs=z_codes[:, cols].bitcast(FP8X4),
                    rhs_scale=z_sc[:, cols],
                    start=True,
                    stop=True,
                )

        late_root(0)
        rounded = []
        for c in range(CHUNKS):
            if c + 1 < CHUNKS:
                late_root(c + 1)
            rounded.append(share(c))
            if c > 0:
                second_product(c - 1, rounded[c - 1])
        second_product(CHUNKS - 1, rounded[-1])

        blocks = H // P
        h_rows, shifts = [], []
        for m in range(blocks):
            h_sb = sb.tile([P, S], F32, name=f"h_sb{m}", align_bytes=64)
            top = sb.tile([P, 1], F32, name=f"top{m}")
            if m == 0:
                kept = S - CHUNK
                top_early = sb.tile([P, 1], F32, name="top_early")
                nc.vector.tensor_scalar(
                    h_sb[:, :kept], h_ps[m][:, :kept], 0.0625, None, ALU.mult, ALU.max, accum_out=top_early[:]
                )
                nc.vector.tensor_scalar(
                    h_sb[:, kept:], h_last[:], 0.0625, top_early[:], ALU.mult, ALU.max, accum_out=top[:]
                )
            else:
                nc.vector.tensor_scalar(h_sb[:], h_ps[m][:], 0.0625, None, ALU.mult, ALU.max, accum_out=top[:])
            shift = sb.tile([P, 1], F32, name=f"shift{m}")
            nc.vector.tensor_scalar(shift[:], top[:], tau_t[:, m : m + 1], -1.0, ALU.mult, ALU.mult)
            h_rows.append(h_sb)
            shifts.append(shift)
        for m in range(blocks):
            h_sb, shift = h_rows[m], shifts[m]
            edges = (0, HALF, S) if m < blocks - 1 else (0, HALF, S - LAST, S)
            for lo, hi in zip(edges, edges[1:]):
                ea = sb.tile([P, hi - lo], F32, name=f"ea{m}_{lo}")
                nc.scalar.activation(
                    ea[:],
                    h_sb[:].indirect(n3_t[:, lo // 16 : hi // 16]),
                    ACT.Exp,
                    bias=shift[:],
                    scale=tau_t[:, m : m + 1],
                )
                res = sb.tile([P, hi - lo], F32, name=f"res{m}_{lo}")
                nc.vector.scalar_tensor_tensor(res[:], h_sb[:, lo:hi], 2.0, ea[:], ALU.mult, ALU.mult)
                nc.sync.dma_start(out[m * P : (m + 1) * P, lo:hi], res[:])
